import numpy as np
CORES = [3,0,2,1,6,7,4,5]
N = 8
T = 24
ROUTE = [[[7,3],[5,2],[5,0],[6,2],[1,5],[5,7],[3,4],[1,4],[1,5],[4,5],[1,4],[5,0],[5,0],[6,3],[4,5],[5,1],[5,0],[5,2],[3,2],[6,5],[3,5],[4,0],[5,1],[5,0]],[[5,6],[5,3],[5,2],[7,2],[2,4],[3,2],[3,6],[1,5],[4,5],[4,7],[5,1],[5,1],[5,3],[1,5],[0,5],[5,2],[5,2],[0,5],[0,5],[7,5],[5,2],[5,1],[6,0],[0,6]],[[5,7],[1,0],[5,1],[7,5],[5,3],[5,7],[3,5],[3,6],[5,3],[5,0],[4,1],[4,6],[5,7],[5,4],[0,4],[4,0],[6,0],[4,5],[5,7],[5,3],[5,2],[7,0],[5,2],[5,3]],[[5,6],[5,0],[5,3],[5,1],[5,1],[5,0],[5,6],[7,3],[1,0],[5,2],[7,1],[7,4],[2,4],[5,3],[5,4],[3,1],[6,5],[6,1],[2,5],[6,5],[2,5],[7,1],[5,4],[5,0]],[[5,3],[1,4],[6,5],[2,3],[2,5],[5,3],[5,1],[5,4],[5,6],[2,5],[0,5],[5,3],[7,5],[5,7],[5,4],[1,2],[7,5],[5,3],[5,3],[1,0],[5,6],[3,5],[4,5],[5,2]],[[6,5],[5,2],[2,5],[5,0],[0,5],[4,5],[2,6],[7,1],[0,5],[5,0],[6,5],[5,6],[1,0],[5,6],[2,0],[7,6],[5,7],[4,5],[0,6],[6,5],[5,6],[4,3],[5,7],[5,3]],[[1,5],[1,5],[5,1],[5,4],[6,5],[2,5],[5,3],[3,5],[5,3],[0,5],[0,5],[1,2],[5,1],[7,3],[4,5],[5,2],[5,7],[1,6],[7,5],[1,5],[1,7],[5,4],[4,3],[5,3]],[[5,0],[5,6],[2,5],[4,3],[2,0],[6,5],[1,5],[5,1],[6,5],[5,6],[5,7],[1,0],[5,6],[7,0],[0,6],[2,5],[5,2],[5,4],[0,1],[5,0],[0,5],[5,7],[3,4],[4,7]]]
YW = 137
def setup_inputs(rng):
    return {"x": rng.standard_normal((N, 128, T), dtype=np.float32)}
def reference(x):
    y = np.full((N, 128, YW), np.nan, x.dtype)
    fill = [0] * N
    for r in range(N):
        for t in range(T):
            for e in ROUTE[r][t]:
                y[e][:, fill[e]] = x[r][:, t]
                fill[e] += 1
    return {"y": y}

@@ -1,0 +1,73 @@
+SCRATCH = {
+    "xs": ("sbuf", [128, 24], "float32"),
+    "pack": ("sbuf", [128, 48], "float32"),
+    "land": ("sbuf", [128, 137], "float32"),
+}
+SEMAPHORES = ["loaded", "packed", "sent", "arrived", "stored"]
+
+ENGINES = 16
+
+
+def runs(cols):
+    out = []
+    for p, c in enumerate(cols):
+        if out and out[-1][1] + out[-1][2] == c:
+            out[-1][2] += 1
+        else:
+            out.append([p, c, 1])
+    return out
+
+
+def rank_program(g, core, T, topo):
+    rank = T.rank_of(core)
+    if rank is None:
+        return
+    route = T.tables["ROUTE"]
+    n_ranks = len(T.cores)
+    toks = [[[t for t, ex in enumerate(route[r]) if e in ex] for e in range(n_ranks)] for r in range(n_ranks)]
+
+    def land_off(e, r):
+        return sum(len(toks[q][e]) for q in range(r))
+
+    g.dma_start(T.xs[:], T.x[:]).then_inc(T.sem.loaded, 16)
+    g.wait_ge(T.sem.loaded, 16)
+
+    n_local = 0
+    base = {}
+    pos = 0
+    for e in range(n_ranks):
+        cols = toks[rank][e]
+        if e == rank:
+            buf, b0 = T.land, land_off(rank, rank)
+        else:
+            buf, b0 = T.pack, pos
+            base[e] = pos
+            pos += len(cols)
+        for p, first, length in runs(cols):
+            g.dma_start(buf[:, b0 + p:b0 + p + length], T.xs[:, first:first + length]).then_inc(T.sem.packed, 16)
+            n_local += 1
+    g.wait_ge(T.sem.packed, 16 * n_local)
+
+    n_sent = 0
+    for k in range(1, n_ranks):
+        e = (rank + k) % n_ranks
+        n = len(toks[rank][e])
+        if n == 0:
+            continue
+        dst = T.cores[e]
+        rid, pid = topo.addr(dst)[:2]
+        o = land_off(e, rank)
+        g.remote_dma(T.land[:, o:o + n], T.pack[:, base[e]:base[e] + n],
+                     remote_sem=T.sem.arrived, local_sem=T.sem.sent,
+                     pid=pid, routing_id=rid, dma_engine_mask=topo.mask(core, dst))
+        n_sent += 1
+
+    n_in = sum(1 for r in range(n_ranks) if r != rank and toks[r][rank])
+    if n_in:
+        g.wait_ge(T.sem.arrived, ENGINES * n_in)
+    if n_sent:
+        g.wait_ge(T.sem.sent, ENGINES * n_sent)
+    count = land_off(rank, n_ranks)
+    if count:
+        g.dma_start(T.y[:, 0:count], T.land[:, 0:count]).then_inc(T.sem.stored, 16)
+        g.wait_ge(T.sem.stored, 16)

@@ -1,11 +1,10 @@
+from concourse.bass import DstId, RemoteDMATransfer
+
 SCRATCH = {
     "xs": ("sbuf", [128, 24], "float32"),
-    "pack": ("sbuf", [128, 48], "float32"),
     "land": ("sbuf", [128, 137], "float32"),
 }
-SEMAPHORES = ["loaded", "packed", "sent", "arrived", "stored"]
-
-ENGINES = 16
+SEMAPHORES = ["loaded", "kept", "sent", "arrived", "stored"]
 
 
 def runs(cols):
@@ -18,56 +17,74 @@ def runs(cols):
     return out
 
 
+def plan(route, r):
+    n_ranks = len(route)
+
+    def toks(q, e):
+        return [t for t, ex in enumerate(route[q]) if e in ex]
+
+    own = []
+    by_run = {}
+    for e in range(n_ranks):
+        off = sum(len(toks(q, e)) for q in range(r))
+        for p, first, width in runs(toks(r, e)):
+            if e == r:
+                own.append((first, width, off + p))
+            else:
+                by_run.setdefault((first, width), []).append((e, off + p))
+    calls = []
+    for w in sorted({width for first, width in by_run}, reverse=True):
+        same = sorted(k for k in by_run if k[1] == w)
+        for i in range(0, len(same), 16):
+            chunk = same[i:i + 16]
+            engines = 16
+            while engines * len(chunk) > 16:
+                engines //= 2
+            calls.append([(first, width, engines, j * engines, by_run[(first, width)])
+                          for j, (first, width) in enumerate(chunk)])
+    return own, calls
+
+
 def rank_program(g, core, T, topo):
     rank = T.rank_of(core)
     if rank is None:
         return
     route = T.tables["ROUTE"]
     n_ranks = len(T.cores)
-    toks = [[[t for t, ex in enumerate(route[r]) if e in ex] for e in range(n_ranks)] for r in range(n_ranks)]
-
-    def land_off(e, r):
-        return sum(len(toks[q][e]) for q in range(r))
+    own, calls = plan(route, rank)
 
     g.dma_start(T.xs[:], T.x[:]).then_inc(T.sem.loaded, 16)
     g.wait_ge(T.sem.loaded, 16)
 
-    n_local = 0
-    base = {}
-    pos = 0
-    for e in range(n_ranks):
-        cols = toks[rank][e]
-        if e == rank:
-            buf, b0 = T.land, land_off(rank, rank)
-        else:
-            buf, b0 = T.pack, pos
-            base[e] = pos
-            pos += len(cols)
-        for p, first, length in runs(cols):
-            g.dma_start(buf[:, b0 + p:b0 + p + length], T.xs[:, first:first + length]).then_inc(T.sem.packed, 16)
-            n_local += 1
-    g.wait_ge(T.sem.packed, 16 * n_local)
-
     n_sent = 0
-    for k in range(1, n_ranks):
-        e = (rank + k) % n_ranks
-        n = len(toks[rank][e])
-        if n == 0:
-            continue
-        dst = T.cores[e]
-        rid, pid = topo.addr(dst)[:2]
-        o = land_off(e, rank)
-        g.remote_dma(T.land[:, o:o + n], T.pack[:, base[e]:base[e] + n],
-                     remote_sem=T.sem.arrived, local_sem=T.sem.sent,
-                     pid=pid, routing_id=rid, dma_engine_mask=topo.mask(core, dst))
-        n_sent += 1
+    for call in calls:
+        transfers = []
+        for first, width, engines, engine0, dests in call:
+            addrs = [topo.addr(T.cores[e]) for e, col in dests]
+            transfers.append(RemoteDMATransfer(
+                dst_ids=[DstId(rid=a[0], pnc=a[1]) for a in addrs],
+                dma_engine_mask=((1 << engines) - 1) << engine0,
+                remote_sem=T.sem.arrived,
+                srcs=[T.xs[:, first:first + width]],
+                dsts=[T.land[:, col:col + width] for e, col in dests]))
+            n_sent += engines
+        g.remote_dma_fused(transfers, local_sem=T.sem.sent)
+    for first, width, col in own:
+        g.dma_start(T.land[:, col:col + width], T.xs[:, first:first + width]).then_inc(T.sem.kept, 16)
 
-    n_in = sum(1 for r in range(n_ranks) if r != rank and toks[r][rank])
+    n_in = 0
+    for r in range(n_ranks):
+        if r != rank:
+            for call in plan(route, r)[1]:
+                for first, width, engines, engine0, dests in call:
+                    n_in += engines * sum(1 for e, col in dests if e == rank)
+    if own:
+        g.wait_ge(T.sem.kept, 16 * len(own))
     if n_in:
-        g.wait_ge(T.sem.arrived, ENGINES * n_in)
+        g.wait_ge(T.sem.arrived, n_in)
     if n_sent:
-        g.wait_ge(T.sem.sent, ENGINES * n_sent)
-    count = land_off(rank, n_ranks)
+        g.wait_ge(T.sem.sent, n_sent)
+    count = sum(1 for q in range(n_ranks) for ex in route[q] if rank in ex)
     if count:
         g.dma_start(T.y[:, 0:count], T.land[:, 0:count]).then_inc(T.sem.stored, 16)
         g.wait_ge(T.sem.stored, 16)

from concourse.bass import DstId, RemoteDMATransfer

SCRATCH = {
    "xs": ("sbuf", [128, 24], "float32"),
    "land": ("sbuf", [128, 137], "float32"),
}
SEMAPHORES = ["loaded", "kept", "sent", "arrived", "stored"]


def runs(cols):
    out = []
    for p, c in enumerate(cols):
        if out and out[-1][1] + out[-1][2] == c:
            out[-1][2] += 1
        else:
            out.append([p, c, 1])
    return out


def plan(route, r):
    n_ranks = len(route)

    def toks(q, e):
        return [t for t, ex in enumerate(route[q]) if e in ex]

    own = []
    by_run = {}
    for e in range(n_ranks):
        off = sum(len(toks(q, e)) for q in range(r))
        for p, first, width in runs(toks(r, e)):
            if e == r:
                own.append((first, width, off + p))
            else:
                by_run.setdefault((first, width), []).append((e, off + p))
    calls = []
    for w in sorted({width for first, width in by_run}, reverse=True):
        same = sorted(k for k in by_run if k[1] == w)
        for i in range(0, len(same), 16):
            chunk = same[i:i + 16]
            engines = 16
            while engines * len(chunk) > 16:
                engines //= 2
            calls.append([(first, width, engines, j * engines, by_run[(first, width)])
                          for j, (first, width) in enumerate(chunk)])
    return own, calls


def rank_program(g, core, T, topo):
    rank = T.rank_of(core)
    if rank is None:
        return
    route = T.tables["ROUTE"]
    n_ranks = len(T.cores)
    own, calls = plan(route, rank)

    g.dma_start(T.xs[:], T.x[:]).then_inc(T.sem.loaded, 16)
    g.wait_ge(T.sem.loaded, 16)

    n_sent = 0
    for call in calls:
        transfers = []
        for first, width, engines, engine0, dests in call:
            addrs = [topo.addr(T.cores[e]) for e, col in dests]
            transfers.append(RemoteDMATransfer(
                dst_ids=[DstId(rid=a[0], pnc=a[1]) for a in addrs],
                dma_engine_mask=((1 << engines) - 1) << engine0,
                remote_sem=T.sem.arrived,
                srcs=[T.xs[:, first:first + width]],
                dsts=[T.land[:, col:col + width] for e, col in dests]))
            n_sent += engines
        g.remote_dma_fused(transfers, local_sem=T.sem.sent)
    for first, width, col in own:
        g.dma_start(T.land[:, col:col + width], T.xs[:, first:first + width]).then_inc(T.sem.kept, 16)

    n_in = 0
    for r in range(n_ranks):
        if r != rank:
            for call in plan(route, r)[1]:
                for first, width, engines, engine0, dests in call:
                    n_in += engines * sum(1 for e, col in dests if e == rank)
    if own:
        g.wait_ge(T.sem.kept, 16 * len(own))
    if n_in:
        g.wait_ge(T.sem.arrived, n_in)
    if n_sent:
        g.wait_ge(T.sem.sent, n_sent)
    count = sum(1 for q in range(n_ranks) for ex in route[q] if rank in ex)
    if count:
        g.dma_start(T.y[:, 0:count], T.land[:, 0:count]).then_inc(T.sem.stored, 16)
        g.wait_ge(T.sem.stored, 16)
